import numpy as np
import ml_dtypes


def mxq(x, axis, fmt="e4m3"):
    dtype, down = {"e4m3": (ml_dtypes.float8_e4m3fn, 7), "e5m2": (ml_dtypes.float8_e5m2, 14)}[fmt]
    v = np.moveaxis(np.asarray(x, np.float32).astype(ml_dtypes.bfloat16).astype(np.float64), axis, -1)
    blocks = v.reshape(v.shape[:-1] + (-1, 32))
    amax = np.abs(blocks).max(-1, keepdims=True)
    byte = np.maximum(np.where(amax > 0, np.frexp(amax)[1] - 1 + 127, 0) - down, 1)
    scale = np.exp2(byte - 127.0)
    codes = (blocks / scale).astype(np.float32).astype(dtype).astype(np.float64)
    return np.moveaxis((codes * scale).reshape(v.shape), -1, axis)


WIDE = False


def mx_kscale(k):
    if not WIDE:
        return np.ones(k)
    levels = np.array([30, -30])
    if k % 512:
        return np.exp2(np.random.permutation(np.resize(levels, k // 32))).repeat(32)
    a = np.empty((k // 512, 16))
    for p in range(k // 512):
        a[p, :8] = np.random.permutation(np.resize(levels, 8))
        for g in range(8):
            far = levels[np.abs(levels - a[p, g]) >= 10]
            a[p, g + 8] = far[np.random.randint(len(far))]
    return np.exp2(a.ravel()).repeat(32)


def f64(x):
    return np.asarray(x).astype(np.float64)


def striped(idx):
    return np.tile(np.asarray(idx).reshape(-1, 16).T, (8, 1)).astype(np.uint16)


def unstriped(offs):
    return offs[:16].T.reshape(-1).astype(np.int64)


E2M1 = np.array([0.0, 0.5, 1.0, 1.5, 2.0, 3.0, 4.0, 6.0, -0.0, -0.5, -1.0, -1.5, -2.0, -3.0, -4.0, -6.0])


def pack_weight(w, fmt):
    k, n = w.shape
    w = f64(np.asarray(w, np.float32).astype(ml_dtypes.bfloat16)).reshape(k // 32, 32, n)
    amax = np.abs(w).max(1)
    if fmt in ("e4m3", "e5m2"):
        byte = np.frexp(amax)[1] - 1 + 127 - (7 if fmt == "e4m3" else 14)
    else:
        mant, ex = np.frexp(amax / 6.0)
        byte = np.where(mant > 0.5, ex, ex - 1) + 127
    byte = np.clip(np.where(amax > 0, byte, 1), 1, 254)
    scaled = (w * np.exp2(127.0 - byte)[:, None, :]).reshape(k, n).astype(np.float32)
    by_word = np.ascontiguousarray(scaled.reshape(k // 512, 128, 4, n).transpose(0, 1, 3, 2))
    if fmt in ("e4m3", "e5m2"):
        words = by_word.astype(ml_dtypes.float8_e4m3fn if fmt == "e4m3" else ml_dtypes.float8_e5m2).view(np.uint8)
    else:
        c = by_word.astype(ml_dtypes.float4_e2m1fn).view(np.uint8) & 0xF
        words = (c[..., 0::2] | (c[..., 1::2] << 4)).reshape(k // 512, 128, 2 * n)
    return np.ascontiguousarray(words), np.ascontiguousarray(byte.astype(np.uint8).reshape(k // 512, 16, n))


def unpack_weight(words, scales, fmt):
    g, _, n = scales.shape
    words = np.ascontiguousarray(words).reshape(g, 128, n, -1)
    if fmt in ("e4m3", "e5m2"):
        vals = words.view(ml_dtypes.float8_e4m3fn if fmt == "e4m3" else ml_dtypes.float8_e5m2).astype(np.float64)
    else:
        nib = np.empty((g, 128, n, 4), np.uint8)
        nib[..., 0::2] = words & 0xF
        nib[..., 1::2] = words >> 4
        vals = E2M1[nib]
    vals = vals * np.repeat(np.exp2(scales.astype(np.float64) - 127.0), 8, axis=1)[..., None]
    return vals.transpose(0, 1, 3, 2).reshape(g * 512, n)


K, T, Z, J, R, Q, N, L, E = 512, 1024, 1024, 256, 512, 1024, 256, 512, 128


def setup_inputs():
    n = np.random.standard_normal
    idx = np.random.permutation(T)[:J]
    idx2 = np.random.permutation(Z)[:J]
    idx3 = np.random.permutation(Q)[:J]
    idx4 = np.random.permutation(J)[:E]
    idx5 = np.random.permutation(J)[:E]
    fk = mx_kscale(K)
    fr = mx_kscale(R)
    fl = mx_kscale(L)
    xtp = pack_weight(n((K, T)) / fk[:, None], "e4m3")
    xop = pack_weight(n((K, Z)) / fk[:, None], "e2m1")
    wp = pack_weight(n((K, R)) * 1 / np.sqrt(K) * fk[:, None] * fr, "e5m2")
    wbp = pack_weight(n((R, N)) * 1 / np.sqrt(R) / fr[:, None], "e5m2")
    sxp = pack_weight(n((L, J)) / fl[:, None], "e2m1")
    wsp = pack_weight(n((L, N)) * 1 / np.sqrt(L) * fl[:, None], "e5m2")
    return {
        "xt_words": xtp[0],
        "xt_scales": xtp[1],
        "xo_words": xop[0],
        "xo_scales": xop[1],
        "w_words": wp[0],
        "w_scales": wp[1],
        "ta": (np.random.uniform(-2.0, 1.0, (R, Q))).astype(np.float32),
        "wb_words": wbp[0],
        "wb_scales": wbp[1],
        "sx_words": sxp[0],
        "sx_scales": sxp[1],
        "ws_words": wsp[0],
        "ws_scales": wsp[1],
        "offs": striped(idx),
        "offs2": striped(idx2),
        "offs3": striped(idx3),
        "offs4": striped(idx4),
        "offs5": striped(idx5),
    }


def reference(xt_words, xt_scales, xo_words, xo_scales, w_words, w_scales, ta, wb_words, wb_scales, sx_words, sx_scales, ws_words, ws_scales, offs, offs2, offs3, offs4, offs5):
    idx = unstriped(offs)
    idx2 = unstriped(offs2)
    idx3 = unstriped(offs3)
    idx4 = unstriped(offs4)
    idx5 = unstriped(offs5)
    xtu = unpack_weight(xt_words, xt_scales, "e4m3")
    xou = unpack_weight(xo_words, xo_scales, "e2m1")
    wu = unpack_weight(w_words, w_scales, "e5m2")
    wbu = unpack_weight(wb_words, wb_scales, "e5m2")
    sxu = unpack_weight(sx_words, sx_scales, "e2m1")
    wsu = unpack_weight(ws_words, ws_scales, "e5m2")
    xtidxg = xtu[:, idx]
    a = wu.T @ xtidxg
    xoidx2g = xou[:, idx2]
    b = wu.T @ xoidx2g
    nm = -np.max(f64(ta), axis=1, keepdims=True)
    hid = np.abs(a - b) * np.exp(f64(ta)[:, idx3] + nm)
    hidq = mxq(hid, 0, "e4m3")
    p = wbu.T @ hidq + wsu.T @ sxu
    y = np.maximum(p[:, idx4], p[:, idx5])
    return y

@@ -1,0 +1,193 @@
+from contextlib import ExitStack
+
+import concourse.mybir as mybir
+from concourse.masks import make_identity
+
+K, T, Z, J, R, Q, N, L, E = 512, 1024, 1024, 256, 512, 1024, 256, 512, 128
+FLOPS = 2 * (2 * K * R * J + R * N * J + L * N * J)
+
+F32 = mybir.dt.float32
+BF16 = mybir.dt.bfloat16
+I32 = mybir.dt.int32
+U32 = mybir.dt.uint32
+U16 = mybir.dt.uint16
+U8 = mybir.dt.uint8
+E4M3 = mybir.dt.float8_e4m3fn_x4
+E5M2 = mybir.dt.float8_e5m2_x4
+E2M1 = mybir.dt.float4_e2m1fn_x4
+ACT = mybir.ActivationFunctionType
+ALU = mybir.AluOpType
+AX = mybir.AxisListType
+
+P = 128
+PACK = 4
+HALVES = J // P
+
+
+def load_scales(queue, plane, scales):
+    for quad in range(4):
+        queue.dma_start(
+            out=plane[32 * quad : 32 * quad + 4, :].bitcast(I32),
+            in_=scales[0, 4 * quad : 4 * quad + 4, :].bitcast(I32),
+        )
+
+
+def load_words8(queue, tile, words):
+    queue.dma_start(out=tile[:].bitcast(I32), in_=words[0].rearrange("p n t -> p (n t)").bitcast(I32))
+
+
+def load_words4(queue, tile, words):
+    queue.dma_start(out=tile[:].bitcast(I32), in_=words[0].bitcast(I32))
+
+
+def tile_list_oneforboth_fading_skip_bestoftwo_kernel(
+    tc, xt_words, xt_scales, xo_words, xo_scales, w_words, w_scales, ta, wb_words, wb_scales,
+    sx_words, sx_scales, ws_words, ws_scales, offs, offs2, offs3, offs4, offs5, out,
+):
+    nc = tc.nc
+    with ExitStack() as ctx:
+        sb = ctx.enter_context(tc.tile_pool(name="sb", bufs=1))
+        ps = ctx.enter_context(tc.psum_pool(name="ps", bufs=1))
+
+        def tile(shape, dtype, name):
+            return sb.tile(shape, dtype, name=name, align_bytes=64)
+
+        list1 = tile([P, J // 16], U16, "list1")
+        list2 = tile([P, J // 16], U16, "list2")
+        list3 = tile([P, J // 16], U16, "list3")
+        list4 = tile([P, E // 16], U16, "list4")
+        list5 = tile([P, E // 16], U16, "list5")
+        xt_w = tile([P, T], U32, "xt_w")
+        xt_s = tile([P, T], U8, "xt_s")
+        xo_w = tile([P, Z], U16, "xo_w")
+        xo_s = tile([P, Z], U8, "xo_s")
+        w_w = tile([P, R], U32, "w_w")
+        w_s = tile([P, R], U8, "w_s")
+        wb_w = tile([P, N], U32, "wb_w")
+        wb_s = tile([P, N], U8, "wb_s")
+        ws_w = tile([P, N], U32, "ws_w")
+        ws_s = tile([P, N], U8, "ws_s")
+        sx_w = tile([P, J], U16, "sx_w")
+        sx_s = tile([P, J], U8, "sx_s")
+        levels = [tile([P, Q], F32, "levels%d" % t) for t in range(PACK)]
+        ident = tile([P, P], F32, "ident")
+        ta_rows = ta.rearrange("(p t) q -> t p q", t=PACK)
+
+        nc.vector.memset(xt_s[:].bitcast(I32), 0)
+        nc.gpsimd.memset(w_s[:].bitcast(I32), 0)
+        nc.vector.memset(xo_s[:].bitcast(I32), 0)
+        for plane in (ws_s, wb_s, sx_s):
+            nc.vector.memset(plane[:].bitcast(I32), 0)
+
+        nc.sync.dma_start(out=levels[0][:], in_=ta_rows[0])
+        nc.sync.dma_start(list1[:], offs)
+        load_words8(nc.sync, xt_w, xt_words)
+        load_scales(nc.scalar, xt_s, xt_scales)
+        load_scales(nc.gpsimd, w_s, w_scales)
+        nc.sync.dma_start(list3[:], offs3)
+        load_words8(nc.sync, w_w, w_words)
+        nc.sync.dma_start(list2[:], offs2)
+        load_words4(nc.sync, xo_w, xo_words)
+        load_scales(nc.sync, xo_s, xo_scales)
+        for t in range(1, PACK):
+            nc.sync.dma_start(out=levels[t][:], in_=ta_rows[t])
+        make_identity(nc, ident[:])
+        load_scales(nc.gpsimd, sx_s, sx_scales)
+        load_words8(nc.sync, ws_w, ws_words)
+        load_words4(nc.sync, sx_w, sx_words)
+        load_words8(nc.sync, wb_w, wb_words)
+        load_scales(nc.sync, ws_s, ws_scales)
+        load_scales(nc.sync, wb_s, wb_scales)
+        nc.sync.dma_start(list4[:], offs4)
+        nc.sync.dma_start(list5[:], offs5)
+
+        neg_max = [tile([P, 1], F32, "neg_max%d" % t) for t in range(PACK)]
+        fade = tile([P, PACK, J], F32, "fade")
+
+        def look(t):
+            nc.vector.tensor_reduce(out=neg_max[t][:], in_=levels[t][:], axis=AX.X, op=ALU.max, negate=True)
+            nc.scalar.activation(
+                out=fade[:, t, :], in_=levels[t][:].indirect(list3[:]), func=ACT.Exp, bias=neg_max[t][:]
+            )
+
+        look(0)
+
+        xtg_w = tile([P, J], U32, "xtg_w")
+        xtg_s = tile([P, J], U8, "xtg_s")
+        xog_w = tile([P, J], U16, "xog_w")
+        xog_s = tile([P, J], U8, "xog_s")
+        nc.vector.tensor_copy(xtg_w[:], xt_w[:].indirect(list1[:]))
+        nc.vector.tensor_copy(xtg_s[:], xt_s[:].indirect(list1[:]))
+        nc.vector.tensor_copy(xog_w[:], xo_w[:].indirect(list2[:]))
+        nc.vector.tensor_copy(xog_s[:], xo_s[:].indirect(list2[:]))
+
+        def first_stage(words, scales, fmt, h, name):
+            cols = slice(h * P, (h + 1) * P)
+            acc = ps.tile([P, R], F32, name=name)
+            nc.tensor.matmul_mx(
+                out=acc[:], lhsT=words[:, cols].bitcast(fmt), lhsT_scale=scales[:, cols],
+                rhs=w_w[:].bitcast(E5M2), rhs_scale=w_s[:], start=True, stop=True,
+            )
+            return acc[:].rearrange("j (m t) -> j t m", t=PACK)
+
+        a_sb = [tile([P, PACK, P], F32, "a_sb%d" % h) for h in range(HALVES)]
+        nb_sb = [tile([P, PACK, P], F32, "nb_sb%d" % h) for h in range(HALVES)]
+        for h in range(HALVES):
+            nc.scalar.copy(out=a_sb[h][:], in_=first_stage(xtg_w, xtg_s, E4M3, h, "a_ps%d" % h))
+        for h in range(HALVES):
+            nc.scalar.activation(
+                out=nb_sb[h][:], in_=first_stage(xog_w, xog_s, E2M1, h, "b_ps%d" % h), func=ACT.Copy, scale=-1.0
+            )
+
+        gap = [tile([P, PACK, P], F32, "gap%d" % h) for h in range(HALVES)]
+        for h in range(HALVES):
+            diff = ps.tile([P, PACK, P], F32, name="diff%d" % h)
+            for t in range(PACK):
+                nc.tensor.matmul(diff[:, t, :], a_sb[h][:, t, :], ident[:], start=True, stop=False, is_transpose=True)
+                nc.tensor.matmul(diff[:, t, :], nb_sb[h][:, t, :], ident[:], start=False, stop=True, is_transpose=True)
+            look(h + 1)
+            nc.scalar.activation(out=gap[h][:], in_=diff[:], func=ACT.Abs)
+        look(3)
+
+        p_ps = [ps.tile([P, J], F32, name="p_ps%d" % u) for u in range(N // P)]
+        for u in range(N // P):
+            cols = slice(u * P, (u + 1) * P)
+            nc.tensor.matmul_mx(
+                out=p_ps[u][:], lhsT=ws_w[:, cols].bitcast(E5M2), lhsT_scale=ws_s[:, cols],
+                rhs=sx_w[:].bitcast(E2M1), rhs_scale=sx_s[:], start=True, stop=False,
+            )
+
+        hid = [tile([P, P, PACK], BF16, "hid%d" % h) for h in range(HALVES)]
+        hid_w = [tile([P, P], U32, "hid_w%d" % h) for h in range(HALVES)]
+        hid_s = [tile([P, P], U8, "hid_s%d" % h) for h in range(HALVES)]
+        for h in range(HALVES):
+            nc.vector.tensor_tensor(
+                out=hid[h][:].rearrange("p (c i) t -> p c t i", i=4),
+                in0=gap[h][:].rearrange("p t (c i) -> p c t i", i=4),
+                in1=fade[:, :, h * P : (h + 1) * P].rearrange("p t (c i) -> p c t i", i=4),
+                op=ALU.mult,
+            )
+        for h in range(HALVES):
+            nc.vector.quantize_mx(
+                out=hid_w[h][:].bitcast(E4M3), scales=hid_s[h][:], in_=hid[h][:].rearrange("p j t -> p (j t)")
+            )
+            for u in range(N // P):
+                cols = slice(u * P, (u + 1) * P)
+                nc.tensor.matmul_mx(
+                    out=p_ps[u][:, h * P : (h + 1) * P], lhsT=wb_w[:, cols].bitcast(E5M2), lhsT_scale=wb_s[:, cols],
+                    rhs=hid_w[h][:].bitcast(E4M3), rhs_scale=hid_s[h][:], start=False, stop=(h == HALVES - 1),
+                )
+
+        p_sb = [tile([P, J], F32, "p_sb%d" % u) for u in range(N // P)]
+        first = [tile([P, E], F32, "first%d" % u) for u in range(N // P)]
+        second = [tile([P, E], F32, "second%d" % u) for u in range(N // P)]
+        best = [tile([P, E], F32, "best%d" % u) for u in range(N // P)]
+        nc.scalar.copy(out=p_sb[0][:], in_=p_ps[0][:])
+        nc.vector.tensor_copy(out=p_sb[1][:], in_=p_ps[1][:])
+        nc.scalar.activation(out=first[0][:], in_=p_sb[0][:].indirect(list4[:]), func=ACT.Copy)
+        nc.scalar.activation(out=second[0][:], in_=p_sb[0][:].indirect(list5[:]), func=ACT.Copy)
+        nc.vector.tensor_copy(first[1][:], p_sb[1][:].indirect(list4[:]))
+        nc.vector.tensor_copy(second[1][:], p_sb[1][:].indirect(list5[:]))
+        for u in (1, 0):
+            nc.vector.tensor_tensor(out=best[u][:], in0=first[u][:], in1=second[u][:], op=ALU.max)
+            nc.sync.dma_start(out=out[u * P : (u + 1) * P, :], in_=best[u][:])

@@ -1,7 +1,6 @@
 from contextlib import ExitStack
 
 import concourse.mybir as mybir
-from concourse.masks import make_identity
 
 K, T, Z, J, R, Q, N, L, E = 512, 1024, 1024, 256, 512, 1024, 256, 512, 128
 FLOPS = 2 * (2 * K * R * J + R * N * J + L * N * J)
@@ -24,12 +23,19 @@ PACK = 4
 HALVES = J // P
 
 
-def load_scales(queue, plane, scales):
-    for quad in range(4):
-        queue.dma_start(
-            out=plane[32 * quad : 32 * quad + 4, :].bitcast(I32),
-            in_=scales[0, 4 * quad : 4 * quad + 4, :].bitcast(I32),
-        )
+def load_scales(queue, plane, scales, quad):
+    queue.dma_start(
+        out=plane[32 * quad : 32 * quad + 4, :].bitcast(I32),
+        in_=scales[0, 4 * quad : 4 * quad + 4, :].bitcast(I32),
+    )
+
+
+def load_scales_filled(queue, plane, scales, quad):
+    rows = scales[0, 4 * quad : 4 * quad + 4, :].bitcast(I32)
+    queue.dma_start(
+        out=plane[32 * quad : 32 * quad + 32, :].bitcast(I32),
+        in_=rows.unsqueeze(0).to_broadcast([8, 4, rows.shape[1]]),
+    )
 
 
 def load_words8(queue, tile, words):
@@ -49,8 +55,8 @@ def tile_list_oneforboth_fading_skip_bestoftwo_kernel(
         sb = ctx.enter_context(tc.tile_pool(name="sb", bufs=1))
         ps = ctx.enter_context(tc.psum_pool(name="ps", bufs=1))
 
-        def tile(shape, dtype, name):
-            return sb.tile(shape, dtype, name=name, align_bytes=64)
+        def tile(shape, dtype, name, tag=None):
+            return sb.tile(shape, dtype, name=name, tag=tag or name, align_bytes=64)
 
         list1 = tile([P, J // 16], U16, "list1")
         list2 = tile([P, J // 16], U16, "list2")
@@ -70,34 +76,51 @@ def tile_list_oneforboth_fading_skip_bestoftwo_kernel(
         sx_w = tile([P, J], U16, "sx_w")
         sx_s = tile([P, J], U8, "sx_s")
         levels = [tile([P, Q], F32, "levels%d" % t) for t in range(PACK)]
-        ident = tile([P, P], F32, "ident")
         ta_rows = ta.rearrange("(p t) q -> t p q", t=PACK)
 
-        nc.vector.memset(xt_s[:].bitcast(I32), 0)
-        nc.gpsimd.memset(w_s[:].bitcast(I32), 0)
+        warm_in = tile([P, 1], F32, "warm_in")
+        warm_out = tile([P, 1], F32, "warm_out")
+        nc.vector.memset(w_s[:].bitcast(I32), 0)
         nc.vector.memset(xo_s[:].bitcast(I32), 0)
-        for plane in (ws_s, wb_s, sx_s):
-            nc.vector.memset(plane[:].bitcast(I32), 0)
-
-        nc.sync.dma_start(out=levels[0][:], in_=ta_rows[0])
+        nc.vector.memset(warm_in[:], 0.0)
+        load_scales_filled(nc.sync, xt_s, xt_scales, 0)
+        load_scales_filled(nc.scalar, xt_s, xt_scales, 1)
+        load_scales_filled(nc.sync, xt_s, xt_scales, 2)
+        load_scales_filled(nc.scalar, xt_s, xt_scales, 3)
         nc.sync.dma_start(list1[:], offs)
-        load_words8(nc.sync, xt_w, xt_words)
-        load_scales(nc.scalar, xt_s, xt_scales)
-        load_scales(nc.gpsimd, w_s, w_scales)
         nc.sync.dma_start(list3[:], offs3)
-        load_words8(nc.sync, w_w, w_words)
+        nc.sync.dma_start(out=levels[0][:], in_=ta_rows[0])
+        load_words8(nc.sync, xt_w, xt_words)
+        nc.scalar.activation(out=warm_out[:], in_=warm_in[:], func=ACT.Exp)
+        load_scales(nc.gpsimd, w_s, w_scales, 3)
+        load_scales(nc.sync, w_s, w_scales, 0)
+        load_scales(nc.sync, w_s, w_scales, 1)
+        load_scales(nc.sync, w_s, w_scales, 2)
         nc.sync.dma_start(list2[:], offs2)
+        nc.sync.dma_start(out=levels[1][:], in_=ta_rows[1])
+        load_words8(nc.sync, w_w, w_words)
         load_words4(nc.sync, xo_w, xo_words)
-        load_scales(nc.sync, xo_s, xo_scales)
-        for t in range(1, PACK):
-            nc.sync.dma_start(out=levels[t][:], in_=ta_rows[t])
-        make_identity(nc, ident[:])
-        load_scales(nc.gpsimd, sx_s, sx_scales)
+        load_scales(nc.sync, xo_s, xo_scales, 0)
+        load_scales(nc.sync, xo_s, xo_scales, 1)
+        load_scales(nc.sync, xo_s, xo_scales, 2)
+        load_scales(nc.sync, xo_s, xo_scales, 3)
+        nc.sync.dma_start(out=levels[2][:], in_=ta_rows[2])
+        nc.sync.dma_start(out=levels[3][:], in_=ta_rows[3])
         load_words8(nc.sync, ws_w, ws_words)
         load_words4(nc.sync, sx_w, sx_words)
         load_words8(nc.sync, wb_w, wb_words)
-        load_scales(nc.sync, ws_s, ws_scales)
-        load_scales(nc.sync, wb_s, wb_scales)
+        load_scales(nc.sync, ws_s, ws_scales, 0)
+        load_scales(nc.sync, ws_s, ws_scales, 1)
+        load_scales(nc.sync, ws_s, ws_scales, 2)
+        load_scales(nc.sync, ws_s, ws_scales, 3)
+        load_scales(nc.sync, sx_s, sx_scales, 0)
+        load_scales(nc.sync, sx_s, sx_scales, 1)
+        load_scales(nc.sync, sx_s, sx_scales, 2)
+        load_scales(nc.sync, sx_s, sx_scales, 3)
+        load_scales(nc.sync, wb_s, wb_scales, 0)
+        load_scales(nc.sync, wb_s, wb_scales, 1)
+        load_scales(nc.sync, wb_s, wb_scales, 2)
+        load_scales(nc.sync, wb_s, wb_scales, 3)
         nc.sync.dma_start(list4[:], offs4)
         nc.sync.dma_start(list5[:], offs5)
 
@@ -109,6 +132,11 @@ def tile_list_oneforboth_fading_skip_bestoftwo_kernel(
             nc.scalar.activation(
                 out=fade[:, t, :], in_=levels[t][:].indirect(list3[:]), func=ACT.Exp, bias=neg_max[t][:]
             )
+
+        wp_w = tile([P, PACK, P], U32, "wp_w")
+        wp_s = tile([P, PACK, P], U8, "wp_s")
+        nc.scalar.copy(out=wp_w[:].rearrange("p t m -> p m t"), in_=w_w[:].rearrange("p (m t) -> p m t", t=PACK))
+        nc.gpsimd.tensor_copy(out=wp_s[:], in_=w_s[:].rearrange("p (m t) -> p t m", t=PACK))
 
         look(0)
 
@@ -123,33 +151,30 @@ def tile_list_oneforboth_fading_skip_bestoftwo_kernel(
 
         def first_stage(words, scales, fmt, h, name):
             cols = slice(h * P, (h + 1) * P)
-            acc = ps.tile([P, R], F32, name=name)
-            nc.tensor.matmul_mx(
-                out=acc[:], lhsT=words[:, cols].bitcast(fmt), lhsT_scale=scales[:, cols],
-                rhs=w_w[:].bitcast(E5M2), rhs_scale=w_s[:], start=True, stop=True,
-            )
-            return acc[:].rearrange("j (m t) -> j t m", t=PACK)
+            acc = ps.tile([P, PACK, P], F32, name=name, tag=name)
+            for t in range(PACK):
+                nc.tensor.matmul_mx(
+                    out=acc[:, t, :], lhsT=wp_w[:, t, :].bitcast(E5M2), lhsT_scale=wp_s[:, t, :],
+                    rhs=words[:, cols].bitcast(fmt), rhs_scale=scales[:, cols], start=True, stop=True,
+                )
+            return acc
 
         a_sb = [tile([P, PACK, P], F32, "a_sb%d" % h) for h in range(HALVES)]
-        nb_sb = [tile([P, PACK, P], F32, "nb_sb%d" % h) for h in range(HALVES)]
         for h in range(HALVES):
-            nc.scalar.copy(out=a_sb[h][:], in_=first_stage(xtg_w, xtg_s, E4M3, h, "a_ps%d" % h))
-        for h in range(HALVES):
-            nc.scalar.activation(
-                out=nb_sb[h][:], in_=first_stage(xog_w, xog_s, E2M1, h, "b_ps%d" % h), func=ACT.Copy, scale=-1.0
-            )
+            nc.scalar.copy(out=a_sb[h][:], in_=first_stage(xtg_w, xtg_s, E4M3, h, "a_ps%d" % h)[:])
+        b_ps = [first_stage(xog_w, xog_s, E2M1, h, "b_ps%d" % h) for h in range(HALVES)]
 
-        gap = [tile([P, PACK, P], F32, "gap%d" % h) for h in range(HALVES)]
-        for h in range(HALVES):
-            diff = ps.tile([P, PACK, P], F32, name="diff%d" % h)
-            for t in range(PACK):
-                nc.tensor.matmul(diff[:, t, :], a_sb[h][:, t, :], ident[:], start=True, stop=False, is_transpose=True)
-                nc.tensor.matmul(diff[:, t, :], nb_sb[h][:, t, :], ident[:], start=False, stop=True, is_transpose=True)
-            look(h + 1)
-            nc.scalar.activation(out=gap[h][:], in_=diff[:], func=ACT.Abs)
+        look(1)
+        look(2)
         look(3)
+        diff = tile([P, HALVES, PACK, P], F32, "diff", tag="levels2")
+        gaps = tile([P, HALVES, PACK, P], F32, "gaps", tag="levels3")
+        gap = [gaps[:, h] for h in range(HALVES)]
+        for h in range(HALVES):
+            nc.vector.tensor_tensor(out=diff[:, h], in0=b_ps[h][:], in1=a_sb[h][:], op=ALU.subtract)
+            nc.scalar.activation(out=gap[h], in_=diff[:, h], func=ACT.Abs)
 
-        p_ps = [ps.tile([P, J], F32, name="p_ps%d" % u) for u in range(N // P)]
+        p_ps = [ps.tile([P, J], F32, name="p_ps%d" % u, tag="b_ps%d" % u) for u in range(N // P)]
         for u in range(N // P):
             cols = slice(u * P, (u + 1) * P)
             nc.tensor.matmul_mx(
@@ -163,7 +188,7 @@ def tile_list_oneforboth_fading_skip_bestoftwo_kernel(
         for h in range(HALVES):
             nc.vector.tensor_tensor(
                 out=hid[h][:].rearrange("p (c i) t -> p c t i", i=4),
-                in0=gap[h][:].rearrange("p t (c i) -> p c t i", i=4),
+                in0=gap[h].rearrange("p t (c i) -> p c t i", i=4),
                 in1=fade[:, :, h * P : (h + 1) * P].rearrange("p t (c i) -> p c t i", i=4),
                 op=ALU.mult,
             )
@@ -184,10 +209,10 @@ def tile_list_oneforboth_fading_skip_bestoftwo_kernel(
         best = [tile([P, E], F32, "best%d" % u) for u in range(N // P)]
         nc.scalar.copy(out=p_sb[0][:], in_=p_ps[0][:])
         nc.vector.tensor_copy(out=p_sb[1][:], in_=p_ps[1][:])
-        nc.scalar.activation(out=first[0][:], in_=p_sb[0][:].indirect(list4[:]), func=ACT.Copy)
-        nc.scalar.activation(out=second[0][:], in_=p_sb[0][:].indirect(list5[:]), func=ACT.Copy)
-        nc.vector.tensor_copy(first[1][:], p_sb[1][:].indirect(list4[:]))
-        nc.vector.tensor_copy(second[1][:], p_sb[1][:].indirect(list5[:]))
+        for u in (0, 1):
+            nc.vector.tensor_copy(first[u][:], p_sb[u][:].indirect(list4[:]))
         for u in (1, 0):
+            nc.scalar.activation(out=second[u][:], in_=p_sb[u][:].indirect(list5[:]), func=ACT.Copy)
+        for u in (0, 1):
             nc.vector.tensor_tensor(out=best[u][:], in0=first[u][:], in1=second[u][:], op=ALU.max)
             nc.sync.dma_start(out=out[u * P : (u + 1) * P, :], in_=best[u][:])

@@ -78,11 +78,8 @@ def tile_list_oneforboth_fading_skip_bestoftwo_kernel(
         levels = [tile([P, Q], F32, "levels%d" % t) for t in range(PACK)]
         ta_rows = ta.rearrange("(p t) q -> t p q", t=PACK)
 
-        warm_in = tile([P, 1], F32, "warm_in")
-        warm_out = tile([P, 1], F32, "warm_out")
         nc.vector.memset(w_s[:].bitcast(I32), 0)
         nc.vector.memset(xo_s[:].bitcast(I32), 0)
-        nc.vector.memset(warm_in[:], 0.0)
         load_scales_filled(nc.sync, xt_s, xt_scales, 0)
         load_scales_filled(nc.scalar, xt_s, xt_scales, 1)
         load_scales_filled(nc.sync, xt_s, xt_scales, 2)
@@ -91,7 +88,6 @@ def tile_list_oneforboth_fading_skip_bestoftwo_kernel(
         nc.sync.dma_start(list3[:], offs3)
         nc.sync.dma_start(out=levels[0][:], in_=ta_rows[0])
         load_words8(nc.sync, xt_w, xt_words)
-        nc.scalar.activation(out=warm_out[:], in_=warm_in[:], func=ACT.Exp)
         load_scales(nc.gpsimd, w_s, w_scales, 3)
         load_scales(nc.sync, w_s, w_scales, 0)
         load_scales(nc.sync, w_s, w_scales, 1)
@@ -135,7 +131,10 @@ def tile_list_oneforboth_fading_skip_bestoftwo_kernel(
 
         wp_w = tile([P, PACK, P], U32, "wp_w")
         wp_s = tile([P, PACK, P], U8, "wp_s")
-        nc.scalar.copy(out=wp_w[:].rearrange("p t m -> p m t"), in_=w_w[:].rearrange("p (m t) -> p m t", t=PACK))
+        nc.scalar.copy(
+            out=wp_w[:].rearrange("p t (c i) -> p c t i", i=4),
+            in_=w_w[:].rearrange("p (c i t) -> p c t i", i=4, t=PACK),
+        )
         nc.gpsimd.tensor_copy(out=wp_s[:], in_=w_s[:].rearrange("p (m t) -> p t m", t=PACK))
 
         look(0)

@@ -173,13 +173,16 @@ def tile_list_oneforboth_fading_skip_bestoftwo_kernel(
             nc.vector.tensor_tensor(out=diff[:, h], in0=b_ps[h][:], in1=a_sb[h][:], op=ALU.subtract)
             nc.scalar.activation(out=gap[h], in_=diff[:, h], func=ACT.Abs)
 
-        p_ps = [ps.tile([P, J], F32, name="p_ps%d" % u, tag="b_ps%d" % u) for u in range(N // P)]
-        for u in range(N // P):
-            cols = slice(u * P, (u + 1) * P)
-            nc.tensor.matmul_mx(
-                out=p_ps[u][:], lhsT=ws_w[:, cols].bitcast(E5M2), lhsT_scale=ws_s[:, cols],
-                rhs=sx_w[:].bitcast(E2M1), rhs_scale=sx_s[:], start=True, stop=False,
-            )
+        p_ps = {}
+        for h in range(HALVES):
+            for u in range(N // P):
+                cols = slice(u * P, (u + 1) * P)
+                p_ps[u, h] = ps.tile([P, P], F32, name="p_ps%d%d" % (u, h), tag="%s_ps%d" % ("ba"[h], u))
+                nc.tensor.matmul_mx(
+                    out=p_ps[u, h][:], lhsT=ws_w[:, cols].bitcast(E5M2), lhsT_scale=ws_s[:, cols],
+                    rhs=sx_w[:, h * P : (h + 1) * P].bitcast(E2M1), rhs_scale=sx_s[:, h * P : (h + 1) * P],
+                    start=True, stop=False,
+                )
 
         hid = [tile([P, P, PACK], BF16, "hid%d" % h) for h in range(HALVES)]
         hid_w = [tile([P, P], U32, "hid_w%d" % h) for h in range(HALVES)]
@@ -198,19 +201,20 @@ def tile_list_oneforboth_fading_skip_bestoftwo_kernel(
             for u in range(N // P):
                 cols = slice(u * P, (u + 1) * P)
                 nc.tensor.matmul_mx(
-                    out=p_ps[u][:, h * P : (h + 1) * P], lhsT=wb_w[:, cols].bitcast(E5M2), lhsT_scale=wb_s[:, cols],
-                    rhs=hid_w[h][:].bitcast(E4M3), rhs_scale=hid_s[h][:], start=False, stop=(h == HALVES - 1),
+                    out=p_ps[u, h][:], lhsT=wb_w[:, cols].bitcast(E5M2), lhsT_scale=wb_s[:, cols],
+                    rhs=hid_w[h][:].bitcast(E4M3), rhs_scale=hid_s[h][:], start=False, stop=True,
                 )
 
         p_sb = [tile([P, J], F32, "p_sb%d" % u) for u in range(N // P)]
         first = [tile([P, E], F32, "first%d" % u) for u in range(N // P)]
         second = [tile([P, E], F32, "second%d" % u) for u in range(N // P)]
         best = [tile([P, E], F32, "best%d" % u) for u in range(N // P)]
-        nc.scalar.copy(out=p_sb[0][:], in_=p_ps[0][:])
-        nc.vector.tensor_copy(out=p_sb[1][:], in_=p_ps[1][:])
+        for h in range(HALVES):
+            for u in (0, 1):
+                nc.scalar.copy(out=p_sb[u][:, h * P : (h + 1) * P], in_=p_ps[u, h][:])
         for u in (0, 1):
             nc.vector.tensor_copy(first[u][:], p_sb[u][:].indirect(list4[:]))
-        for u in (1, 0):
+        for u in (0, 1):
             nc.scalar.activation(out=second[u][:], in_=p_sb[u][:].indirect(list5[:]), func=ACT.Copy)
         for u in (0, 1):
             nc.vector.tensor_tensor(out=best[u][:], in0=first[u][:], in1=second[u][:], op=ALU.max)

from contextlib import ExitStack

import concourse.mybir as mybir

K, T, Z, J, R, Q, N, L, E = 512, 1024, 1024, 256, 512, 1024, 256, 512, 128
FLOPS = 2 * (2 * K * R * J + R * N * J + L * N * J)

F32 = mybir.dt.float32
BF16 = mybir.dt.bfloat16
I32 = mybir.dt.int32
U32 = mybir.dt.uint32
U16 = mybir.dt.uint16
U8 = mybir.dt.uint8
E4M3 = mybir.dt.float8_e4m3fn_x4
E5M2 = mybir.dt.float8_e5m2_x4
E2M1 = mybir.dt.float4_e2m1fn_x4
ACT = mybir.ActivationFunctionType
ALU = mybir.AluOpType
AX = mybir.AxisListType

P = 128
PACK = 4
HALVES = J // P


def load_scales(queue, plane, scales, quad):
    queue.dma_start(
        out=plane[32 * quad : 32 * quad + 4, :].bitcast(I32),
        in_=scales[0, 4 * quad : 4 * quad + 4, :].bitcast(I32),
    )


def load_scales_filled(queue, plane, scales, quad):
    rows = scales[0, 4 * quad : 4 * quad + 4, :].bitcast(I32)
    queue.dma_start(
        out=plane[32 * quad : 32 * quad + 32, :].bitcast(I32),
        in_=rows.unsqueeze(0).to_broadcast([8, 4, rows.shape[1]]),
    )


def load_words8(queue, tile, words):
    queue.dma_start(out=tile[:].bitcast(I32), in_=words[0].rearrange("p n t -> p (n t)").bitcast(I32))


def load_words4(queue, tile, words):
    queue.dma_start(out=tile[:].bitcast(I32), in_=words[0].bitcast(I32))


def tile_list_oneforboth_fading_skip_bestoftwo_kernel(
    tc, xt_words, xt_scales, xo_words, xo_scales, w_words, w_scales, ta, wb_words, wb_scales,
    sx_words, sx_scales, ws_words, ws_scales, offs, offs2, offs3, offs4, offs5, out,
):
    nc = tc.nc
    with ExitStack() as ctx:
        sb = ctx.enter_context(tc.tile_pool(name="sb", bufs=1))
        ps = ctx.enter_context(tc.psum_pool(name="ps", bufs=1))

        def tile(shape, dtype, name, tag=None):
            return sb.tile(shape, dtype, name=name, tag=tag or name, align_bytes=64)

        list1 = tile([P, J // 16], U16, "list1")
        list2 = tile([P, J // 16], U16, "list2")
        list3 = tile([P, J // 16], U16, "list3")
        list4 = tile([P, E // 16], U16, "list4")
        list5 = tile([P, E // 16], U16, "list5")
        xt_w = tile([P, T], U32, "xt_w")
        xt_s = tile([P, T], U8, "xt_s")
        xo_w = tile([P, Z], U16, "xo_w")
        xo_s = tile([P, Z], U8, "xo_s")
        w_w = tile([P, R], U32, "w_w")
        w_s = tile([P, R], U8, "w_s")
        wb_w = tile([P, N], U32, "wb_w")
        wb_s = tile([P, N], U8, "wb_s")
        ws_w = tile([P, N], U32, "ws_w")
        ws_s = tile([P, N], U8, "ws_s")
        sx_w = tile([P, J], U16, "sx_w")
        sx_s = tile([P, J], U8, "sx_s")
        levels = [tile([P, Q], F32, "levels%d" % t) for t in range(PACK)]
        ta_rows = ta.rearrange("(p t) q -> t p q", t=PACK)

        nc.vector.memset(w_s[:].bitcast(I32), 0)
        nc.vector.memset(xo_s[:].bitcast(I32), 0)
        load_scales_filled(nc.sync, xt_s, xt_scales, 0)
        load_scales_filled(nc.scalar, xt_s, xt_scales, 1)
        load_scales_filled(nc.sync, xt_s, xt_scales, 2)
        load_scales_filled(nc.scalar, xt_s, xt_scales, 3)
        nc.sync.dma_start(list1[:], offs)
        nc.sync.dma_start(list3[:], offs3)
        nc.sync.dma_start(out=levels[0][:], in_=ta_rows[0])
        load_words8(nc.sync, xt_w, xt_words)
        load_scales(nc.gpsimd, w_s, w_scales, 3)
        load_scales(nc.sync, w_s, w_scales, 0)
        load_scales(nc.sync, w_s, w_scales, 1)
        load_scales(nc.sync, w_s, w_scales, 2)
        nc.sync.dma_start(list2[:], offs2)
        nc.sync.dma_start(out=levels[1][:], in_=ta_rows[1])
        load_words8(nc.sync, w_w, w_words)
        load_words4(nc.sync, xo_w, xo_words)
        load_scales(nc.sync, xo_s, xo_scales, 0)
        load_scales(nc.sync, xo_s, xo_scales, 1)
        load_scales(nc.sync, xo_s, xo_scales, 2)
        load_scales(nc.sync, xo_s, xo_scales, 3)
        nc.sync.dma_start(out=levels[2][:], in_=ta_rows[2])
        nc.sync.dma_start(out=levels[3][:], in_=ta_rows[3])
        load_words8(nc.sync, ws_w, ws_words)
        load_words4(nc.sync, sx_w, sx_words)
        load_words8(nc.sync, wb_w, wb_words)
        load_scales(nc.sync, ws_s, ws_scales, 0)
        load_scales(nc.sync, ws_s, ws_scales, 1)
        load_scales(nc.sync, ws_s, ws_scales, 2)
        load_scales(nc.sync, ws_s, ws_scales, 3)
        load_scales(nc.sync, sx_s, sx_scales, 0)
        load_scales(nc.sync, sx_s, sx_scales, 1)
        load_scales(nc.sync, sx_s, sx_scales, 2)
        load_scales(nc.sync, sx_s, sx_scales, 3)
        load_scales(nc.sync, wb_s, wb_scales, 0)
        load_scales(nc.sync, wb_s, wb_scales, 1)
        load_scales(nc.sync, wb_s, wb_scales, 2)
        load_scales(nc.sync, wb_s, wb_scales, 3)
        nc.sync.dma_start(list4[:], offs4)
        nc.sync.dma_start(list5[:], offs5)

        neg_max = [tile([P, 1], F32, "neg_max%d" % t) for t in range(PACK)]
        fade = tile([P, PACK, J], F32, "fade")

        def look(t):
            nc.vector.tensor_reduce(out=neg_max[t][:], in_=levels[t][:], axis=AX.X, op=ALU.max, negate=True)
            nc.scalar.activation(
                out=fade[:, t, :], in_=levels[t][:].indirect(list3[:]), func=ACT.Exp, bias=neg_max[t][:]
            )

        wp_w = tile([P, PACK, P], U32, "wp_w")
        wp_s = tile([P, PACK, P], U8, "wp_s")
        nc.scalar.copy(
            out=wp_w[:].rearrange("p t (c i) -> p c t i", i=4),
            in_=w_w[:].rearrange("p (c i t) -> p c t i", i=4, t=PACK),
        )
        nc.gpsimd.tensor_copy(out=wp_s[:], in_=w_s[:].rearrange("p (m t) -> p t m", t=PACK))

        look(0)

        xtg_w = tile([P, J], U32, "xtg_w")
        xtg_s = tile([P, J], U8, "xtg_s")
        xog_w = tile([P, J], U16, "xog_w")
        xog_s = tile([P, J], U8, "xog_s")
        nc.vector.tensor_copy(xtg_w[:], xt_w[:].indirect(list1[:]))
        nc.vector.tensor_copy(xtg_s[:], xt_s[:].indirect(list1[:]))
        nc.vector.tensor_copy(xog_w[:], xo_w[:].indirect(list2[:]))
        nc.vector.tensor_copy(xog_s[:], xo_s[:].indirect(list2[:]))

        def first_stage(words, scales, fmt, h, name):
            cols = slice(h * P, (h + 1) * P)
            acc = ps.tile([P, PACK, P], F32, name=name, tag=name)
            for t in range(PACK):
                nc.tensor.matmul_mx(
                    out=acc[:, t, :], lhsT=wp_w[:, t, :].bitcast(E5M2), lhsT_scale=wp_s[:, t, :],
                    rhs=words[:, cols].bitcast(fmt), rhs_scale=scales[:, cols], start=True, stop=True,
                )
            return acc

        a_sb = [tile([P, PACK, P], F32, "a_sb%d" % h) for h in range(HALVES)]
        for h in range(HALVES):
            nc.scalar.copy(out=a_sb[h][:], in_=first_stage(xtg_w, xtg_s, E4M3, h, "a_ps%d" % h)[:])
        b_ps = [first_stage(xog_w, xog_s, E2M1, h, "b_ps%d" % h) for h in range(HALVES)]

        look(1)
        look(2)
        look(3)
        diff = tile([P, HALVES, PACK, P], F32, "diff", tag="levels2")
        gaps = tile([P, HALVES, PACK, P], F32, "gaps", tag="levels3")
        gap = [gaps[:, h] for h in range(HALVES)]
        for h in range(HALVES):
            nc.vector.tensor_tensor(out=diff[:, h], in0=b_ps[h][:], in1=a_sb[h][:], op=ALU.subtract)
            nc.scalar.activation(out=gap[h], in_=diff[:, h], func=ACT.Abs)

        p_ps = {}
        for h in range(HALVES):
            for u in range(N // P):
                cols = slice(u * P, (u + 1) * P)
                p_ps[u, h] = ps.tile([P, P], F32, name="p_ps%d%d" % (u, h), tag="%s_ps%d" % ("ba"[h], u))
                nc.tensor.matmul_mx(
                    out=p_ps[u, h][:], lhsT=ws_w[:, cols].bitcast(E5M2), lhsT_scale=ws_s[:, cols],
                    rhs=sx_w[:, h * P : (h + 1) * P].bitcast(E2M1), rhs_scale=sx_s[:, h * P : (h + 1) * P],
                    start=True, stop=False,
                )

        hid = [tile([P, P, PACK], BF16, "hid%d" % h) for h in range(HALVES)]
        hid_w = [tile([P, P], U32, "hid_w%d" % h) for h in range(HALVES)]
        hid_s = [tile([P, P], U8, "hid_s%d" % h) for h in range(HALVES)]
        for h in range(HALVES):
            nc.vector.tensor_tensor(
                out=hid[h][:].rearrange("p (c i) t -> p c t i", i=4),
                in0=gap[h].rearrange("p t (c i) -> p c t i", i=4),
                in1=fade[:, :, h * P : (h + 1) * P].rearrange("p t (c i) -> p c t i", i=4),
                op=ALU.mult,
            )
        for h in range(HALVES):
            nc.vector.quantize_mx(
                out=hid_w[h][:].bitcast(E4M3), scales=hid_s[h][:], in_=hid[h][:].rearrange("p j t -> p (j t)")
            )
            for u in range(N // P):
                cols = slice(u * P, (u + 1) * P)
                nc.tensor.matmul_mx(
                    out=p_ps[u, h][:], lhsT=wb_w[:, cols].bitcast(E5M2), lhsT_scale=wb_s[:, cols],
                    rhs=hid_w[h][:].bitcast(E4M3), rhs_scale=hid_s[h][:], start=False, stop=True,
                )

        p_sb = [tile([P, J], F32, "p_sb%d" % u) for u in range(N // P)]
        first = [tile([P, E], F32, "first%d" % u) for u in range(N // P)]
        second = [tile([P, E], F32, "second%d" % u) for u in range(N // P)]
        best = [tile([P, E], F32, "best%d" % u) for u in range(N // P)]
        for h in range(HALVES):
            for u in (0, 1):
                nc.scalar.copy(out=p_sb[u][:, h * P : (h + 1) * P], in_=p_ps[u, h][:])
        for u in (0, 1):
            nc.vector.tensor_copy(first[u][:], p_sb[u][:].indirect(list4[:]))
        for u in (0, 1):
            nc.scalar.activation(out=second[u][:], in_=p_sb[u][:].indirect(list5[:]), func=ACT.Copy)
        for u in (0, 1):
            nc.vector.tensor_tensor(out=best[u][:], in0=first[u][:], in1=second[u][:], op=ALU.max)
            nc.sync.dma_start(out=out[u * P : (u + 1) * P, :], in_=best[u][:])
